import numpy as np
import ml_dtypes


def mxq(x, axis, fmt="e4m3"):
    dtype, down = {"e4m3": (ml_dtypes.float8_e4m3fn, 7), "e5m2": (ml_dtypes.float8_e5m2, 14)}[fmt]
    v = np.moveaxis(np.asarray(x, np.float32).astype(ml_dtypes.bfloat16).astype(np.float64), axis, -1)
    blocks = v.reshape(v.shape[:-1] + (-1, 32))
    amax = np.abs(blocks).max(-1, keepdims=True)
    byte = np.maximum(np.where(amax > 0, np.frexp(amax)[1] - 1 + 127, 0) - down, 1)
    scale = np.exp2(byte - 127.0)
    codes = (blocks / scale).astype(np.float32).astype(dtype).astype(np.float64)
    return np.moveaxis((codes * scale).reshape(v.shape), -1, axis)


WIDE = False


def mx_kscale(k):
    if not WIDE:
        return np.ones(k)
    levels = np.array([10, -10, 5, -5, 0])
    if k % 512:
        return np.exp2(np.random.permutation(np.resize(levels, k // 32))).repeat(32)
    a = np.empty((k // 512, 16))
    for p in range(k // 512):
        a[p, :8] = np.random.permutation(np.resize(levels, 8))
        for g in range(8):
            far = levels[np.abs(levels - a[p, g]) >= 10]
            a[p, g + 8] = far[np.random.randint(len(far))]
    return np.exp2(a.ravel()).repeat(32)


BF16 = ml_dtypes.bfloat16


def bf(x):
    return np.asarray(x, np.float32).astype(BF16)


def f64(x):
    return np.asarray(x).astype(np.float64)


M, K, D, H, R = 2048, 1024, 512, 8, 512
C = D // H
C2 = C // 2
EPS = 1e-5


def rotate(k, cos, sin):
    kh = k.reshape(M, H, C)
    k1, k2 = kh[:, :, :C2], kh[:, :, C2:]
    c, s = cos[:, None, :], sin[:, None, :]
    return np.concatenate([k1 * c - k2 * s, k2 * c + k1 * s], axis=2).reshape(M, D)


def head_norm(y, gain):
    yh = y.reshape(R, H, C)
    r = np.sqrt(np.mean(yh * yh, axis=2, keepdims=True) + EPS)
    return (yh / r).reshape(R, D) * gain


def draw0():
    s, u = mx_kscale(K), mx_kscale(M)
    phase = np.random.uniform(-np.pi, np.pi, (M, C2))
    return {"x": bf(np.random.standard_normal((M, K)) * s * u[:, None]),
            "wk": bf(np.random.standard_normal((K, D)) / np.sqrt(K) / s[:, None]),
            "wv": bf(np.random.standard_normal((K, D)) / np.sqrt(K) / s[:, None]),
            "rope_cos": bf(np.cos(phase)),
            "rope_sin": bf(np.sin(phase)),
            "v0": bf(np.random.standard_normal((M, D)) * u[:, None]),
            "lam": bf(np.random.uniform(0.3, 0.7, D)),
            "e": bf(np.random.standard_normal((R, M)) / np.sqrt(M) / u),
            "f": bf(np.random.standard_normal((R, M)) / np.sqrt(M) / u),
            "e_bias": bf(0.3 * np.random.standard_normal(R)),
            "f_bias": bf(0.3 * np.random.standard_normal(R)),
            "gain": bf(1 + 0.1 * np.random.standard_normal(D))}


def core(x, wk, wv, rope_cos, rope_sin, v0, lam, e, f, e_bias, f_bias, gain):
    xq = mxq(f64(x), 1, "e4m3")
    k = xq @ mxq(f64(wk), 0, "e4m3")
    v = xq @ mxq(f64(wv), 0, "e4m3")
    kr = rotate(k, f64(rope_cos), f64(rope_sin))
    mix = f64(lam)
    vm = mix * v + (1 - mix) * f64(v0)
    ks = mxq(f64(e), 1, "e4m3") @ mxq(kr, 0, "e4m3")
    vs = mxq(f64(f), 1, "e4m3") @ mxq(vm, 0, "e4m3")
    keys = head_norm(ks + f64(e_bias)[:, None], f64(gain))
    values = vs + f64(f_bias)[:, None]
    return keys, values


def e4m3fn_bytes(y):
    return np.clip(np.asarray(y, np.float64), -448.0, 448.0).astype(np.float32).astype(ml_dtypes.float8_e4m3fn).view(np.uint8)


def e4m3fn_values(b):
    return np.asarray(b, np.uint8).view(ml_dtypes.float8_e4m3fn).astype(np.float64)


def setup_inputs():
    d = draw0()
    x0 = np.asarray(d['f']).astype(np.float64)
    s = (np.max(np.abs(x0), axis=(0,), keepdims=True) / 448.0).astype(np.float32)
    out = {}
    for k, v in d.items():
        if k == 'f':
            out['f_bytes'] = e4m3fn_bytes(x0 / s.astype(np.float64))
            out['f_scale'] = s
        else:
            out[k] = v
    return out


def reference(x, wk, wv, rope_cos, rope_sin, v0, lam, e, f_bytes, f_scale, e_bias, f_bias, gain):
    return core(x, wk, wv, rope_cos, rope_sin, v0, lam, e, e4m3fn_values(f_bytes) * f_scale.astype(np.float64), e_bias, f_bias, gain)

from contextlib import ExitStack

import concourse.mybir as mybir
from concourse.masks import make_identity

M, K, D, H, R = 2048, 1024, 512, 8, 512
C = D // H
EPS = 1e-5
P = 128
GROUPS = M // 512
PASSES = K // 512
SLOT_TILES = R // P
GRP_BUFS = {"x": 3, "f": 2, "kr": 2, "vm": 1}
FLOPS = 2 * M * K * 2 * D + 2 * 2 * R * M * D

F32 = mybir.dt.float32
BF16 = mybir.dt.bfloat16
U32 = mybir.dt.uint32
U8 = mybir.dt.uint8
FP8 = mybir.dt.float8_e4m3fn
FP8X4 = mybir.dt.float8_e4m3fn_x4
ALU = mybir.AluOpType
ACTF = mybir.ActivationFunctionType
AX = mybir.AxisListType


ORDER = """
ld_x0:0 ld_small:4 ld_x0:1 ld_wk:0 ld_f:0 ld_v0:0 x_turn:0:0:0 x_copy:0:0:0 x_turn:0:0:1 ld_wk:1 
x_copy:0:0:1 x_turn:0:1:0 x_copy:0:1:0 x_turn:0:1:1 x_copy:0:1:1 f_wid:0 ld_small:0 ld_f:3 ld_small:3 
v0_turn:0:1 ld_wv:0 f_turn:0:0 ld_e:0 x_q:0:0 v0_turn:0:0 w_pack_k:0:0 x_q:0:1 ld_small:5 f_wid:3 
w_pack_v:0:0 ld_wv:1 f_turn:3:0 w_pack_k:0:1 w_q_k:0 w_pack_v:0:1 f_turn:0:1 f_turn:3:1 e_turn:0:1 
w_pack_k:1:0 ld_f:1 w_pack_k:1:1 e_turn:0:0 w_q_k:1 k_mm:0:0 ld_v0:2 f_mul:0:0 f_mul:0:1 k_mm:0:1 
k_mm:0:2 ld_small:1 columns ld_small:2 k_mm:0:3 f_mul:3:0 f_mul:3:1 v0_scale:0:1 v0_scale:0:0 ld_v0:1 
ld_x:1 x_turn:1:0:0 x_turn:1:0:1 x_turn:1:1:0 x_turn:1:1:1 ld_e:2 tables e_copy:0:0 e_copy:0:1 ld_x:3 
f_q:0 w_q_v:0 w_pack_v:1:0 f_q:3 k_mul:0:0 w_pack_v:1:1 k_mul:0:1 k_mul:0:2 k_mul:0:3 e_turn:2:1 ld_x:2 
w_q_v:1 e_q:0 x_copy:1:0:0 x_copy:1:0:1 e_turn:2:0 k_add:0:0 x_copy:1:1:0 v_mm:0:0 v_mm:0:1 v_mm:0:2 
v_mm:0:3 x_copy:1:1:1 x_turn:2:0:0 e_copy:2:0 e_copy:2:1 x_turn:2:0:1 x_turn:2:1:0 x_turn:2:1:1 v_mix:0:0 
k_add:0:1 v_mix:0:1 v_mix:0:2 v_mix:0:3 x_q:1:0 ld_small:6 x_q:1:1 x_copy:2:0:0 x_copy:2:0:1 x_copy:2:1:0 
k_mm:1:0 x_copy:2:1:1 x_turn:3:0:0 x_turn:3:0:1 k_mm:1:1 x_turn:3:1:0 x_turn:3:1:1 v0_turn:1:1 k_mm:1:2 
x_copy:3:0:0 x_copy:3:0:1 k_mm:1:3 e_q:2 x_copy:3:1:0 v0_turn:1:0 x_copy:3:1:1 v0_scale:1:1 v0_scale:1:0 
v0_turn:2:1 ld_e:1 x_q:2:0 kr_q:0 f_wid:1 ld_e:3 k_mul:1:0 x_q:2:1 v0_turn:2:0 v_mm:1:0 v_mm:1:1 x_q:3:0 
v_mm:1:2 v_mm:1:3 k_mul:1:1 k_mm:2:0 x_q:3:1 k_mul:1:2 k_mm:2:1 k_mul:1:3 ld_f:2 k_add:1:0 v_mix:1:0 
vm_turn:0:0 k_mm:2:2 v_mix:1:1 e_turn:3:1 v_mix:1:2 v0_scale:2:1 vm_turn:0:1 v0_scale:2:0 k_add:1:1 
k_mm:2:3 v_mix:1:3 e_turn:3:0 vm_copy:0:0 k_mul:2:0 v_mm:2:0 v_mm:2:1 v_mm:2:2 e_turn:1:1 v_mm:2:3 
k_mm:3:0 k_mul:2:1 ld_v0:3 kr_q:1 k_mul:2:2 k_mm:3:1 e_turn:1:0 k_mul:2:3 vm_turn:1:0 vm_copy:0:1 
k_add:2:0 k_mm:3:2 vm_turn:1:1 e_copy:3:0 e_copy:3:1 k_mm:3:3 v_mix:2:0 k_add:2:1 f_wid:2 f_turn:1:0 
e_copy:1:0 v_mix:2:1 e_copy:1:1 v_mix:2:2 vm_q:0 v_mix:2:3 v0_turn:3:1 vm_copy:1:0 k_mul:3:0 kr_q:2 
k_mul:3:1 f_turn:1:1 v0_turn:3:0 e_q:3 k_mul:3:2 k_mul:3:3 vm_copy:1:1 vm_turn:2:0 vm_turn:2:1 f_mul:1:0 
f_mul:1:1 v0_scale:3:1 v0_scale:3:0 v_mm:3:0 v_mm:3:1 v_mm:3:2 v_mm:3:3 k_add:3:0 v_mix:3:0 f_turn:2:0 
v_mix:3:1 v_mix:3:2 k_add:3:1 vm_copy:2:0 e_q:1 vm_q:1 kr_q:3 v_mix:3:3 f_q:1 f_turn:2:1 vm_copy:2:1 
vm_q:2 ks_mm:0 ks_mm:1 ks_sq:0 ks_mm:2 ks_mm:3 ks_read:0 vm_turn:3:0 vs_mm:0:0 vm_turn:3:1 ks_sq:1 
f_mul:2:0 ks_read:1 vs_mm:1:0 f_mul:2:1 ks_norm:0 ks_rec:0 vs_mm:0:1 ks_read:2 vs_mm:2:0 ks_sq:2 
ks_norm:1 ks_out:0 vs_mm:1:1 ks_read:3 ks_rec:1 vs_mm:3:0 ks_norm:2 ks_sq:3 vs_mm:2:1 vm_copy:3:0 f_q:2 
ks_rec:2 ks_norm:3 vs_mm:3:1 ks_out:1 vm_copy:3:1 ks_rec:3 vm_q:3 ks_out:2 vs_mm:0:2 ks_out:3 vs_mm:0:3 
vs_out:0 vs_mm:1:2 vs_mm:1:3 vs_out:1 vs_mm:2:2 vs_mm:2:3 vs_out:2 vs_mm:3:2 vs_mm:3:3 vs_out:3 
"""


def ADD_ENGINE(g, hp):
    return True


def F_ACT(g):
    return g in ()


def F_ENGINE(g, ap):
    return 'scalar'


KO = 'dve'


def VS_ACT(a):
    return a % 2 == 0


F_FINE = False
W_ENGINE = {('k', 0, 0): 'vector', ('k', 1, 0): 'vector', ('v', 0, 0): 'scalar', ('v', 1, 0): 'scalar', ('k', 0, 1): 'vector', ('k', 1, 1): 'vector', ('v', 0, 1): 'scalar', ('v', 1, 1): 'scalar'}


def tile_linformer_token_shortening_f4_kernel(
    tc, x, wk, wv, rope_cos, rope_sin, v0, lam, e, f_bytes, f_scale, e_bias, f_bias, gain, out_0, out_1
):
    nc = tc.nc
    with ExitStack() as ctx:
        keep = ctx.enter_context(tc.tile_pool(name="keep", bufs=1))
        loads = ctx.enter_context(tc.tile_pool(name="loads", bufs=2))
        work = ctx.enter_context(tc.tile_pool(name="work", bufs=2))
        psum = ctx.enter_context(tc.psum_pool(name="psum", bufs=2))

        ctx.enter_context(tc.manual_schedule())

        x_g = x.rearrange("(g m t) k -> g m t k", m=P, t=4)
        v0_g = v0.rearrange("(g m t) d -> g m t d", m=P, t=4)
        e_g = e.rearrange("(p a) (g k) -> g p a k", a=SLOT_TILES, k=512)
        f_g = f_bytes.rearrange("(p a) (g k) -> g p a k", a=SLOT_TILES, k=512)
        cos_g = rope_cos.rearrange("(g m t) j -> m g t j", m=P, t=4)
        sin_g = rope_sin.rearrange("(g m t) j -> m g t j", m=P, t=4)

        f_raw = [None] * GROUPS
        x_sb = [None] * GROUPS
        v0_sb = [None] * GROUPS
        e_sb = [None] * GROUPS
        w_raw = {}

        def load_f(g):
            f_raw_t = loads.tile([P, SLOT_TILES, 512], U8, name="f_raw", bufs=4)
            nc.sync.dma_start(out=f_raw_t[:], in_=f_g[g])
            f_raw[g] = f_raw_t

        def load_x(g):
            x_t = loads.tile([P, 4, K], BF16, name="x_sb", bufs=3, align_bytes=64)
            nc.sync.dma_start(out=x_t[:], in_=x_g[g])
            x_sb[g] = x_t

        def load_x0(kk):
            if kk == 0:
                x_t = loads.tile([P, 4, K], BF16, name="x_sb", bufs=3, align_bytes=64)
                x_sb[0] = x_t
            cols = slice(kk * 512, (kk + 1) * 512)
            nc.sync.dma_start(out=x_sb[0][:, :, cols], in_=x_g[0][:, :, cols])

        def load_w(name, w, kk):
            if kk == 0:
                w_t = loads.tile([P, PASSES, 4, D], BF16, name="w_raw", bufs=2, align_bytes=64)
                w_raw[name] = w_t
            src = w.rearrange("(kk p j) c -> kk p j c", p=P, j=4)[kk]
            nc.sync.dma_start(out=w_raw[name][:, kk], in_=src)

        def load_v0(g):
            v0_t = loads.tile([P, 4, D], BF16, name="v0_sb", bufs=2, align_bytes=64)
            nc.sync.dma_start(out=v0_t[:], in_=v0_g[g])
            v0_sb[g] = v0_t

        def load_e(g):
            e_t = loads.tile([P, SLOT_TILES, 512], BF16, name="e_sb", bufs=2, align_bytes=64)
            nc.sync.dma_start(out=e_t[:], in_=e_g[g])
            e_sb[g] = e_t

        fsc = keep.tile([P, GROUPS, 4], F32, name="fsc")
        cos_raw = keep.tile([P, GROUPS, 4, 32], BF16, name="cos_raw")
        sin_raw = keep.tile([P, GROUPS, 4, 32], BF16, name="sin_raw")
        lam_raw = keep.tile([P, 2, 2], BF16, name="lam_raw")
        eb_raw = keep.tile([P, SLOT_TILES], BF16, name="eb_raw")
        fb_raw = keep.tile([P, SLOT_TILES], BF16, name="fb_raw")
        gain_sb = keep.tile([P, D], BF16, name="gain_sb")

        loaders = dict(
            f=load_f, x=load_x, v0=load_v0, e=load_e, wk=lambda i: load_w("k", wk, i), wv=lambda i: load_w("v", wv, i), x0=load_x0,
            small=lambda i: [
                lambda: nc.sync.dma_start(out=fsc[:], in_=f_scale.rearrange("o (g p t) -> p (o g) t", p=P, t=4)),
                lambda: nc.sync.dma_start(out=cos_raw[:], in_=cos_g),
                lambda: nc.sync.dma_start(out=sin_raw[:], in_=sin_g),
                lambda: nc.sync.dma_start(out=lam_raw[:], in_=lam.rearrange("(dd w i) -> w dd i", dd=2, i=2)),
                lambda: nc.sync.dma_start(out=eb_raw[:], in_=e_bias.rearrange("(p a) -> p a", a=SLOT_TILES)),
                lambda: nc.sync.dma_start(out=fb_raw[:], in_=f_bias.rearrange("(p a) -> p a", a=SLOT_TILES)),
                lambda: nc.sync.dma_start(out=gain_sb[:], in_=gain.partition_broadcast(P)),
            ][i](),
        )

        ident = keep.tile([P, P], F32, name="ident")
        make_identity(nc, ident[:])
        warm = keep.tile([P, 1], F32, name="warm")
        nc.vector.memset(warm[:], 1.0)
        nc.scalar.activation(warm[:], warm[:], ACTF.Sqrt)
        eps_col = keep.tile([P, 1], F32, name="eps_col")
        nc.vector.tensor_scalar(eps_col[:], warm[:], 0.0, EPS, op0=ALU.mult, op1=ALU.add)

        lamf = keep.tile([P, 4], F32, name="lamf")
        oml = keep.tile([P, 4], F32, name="oml")
        ebf = keep.tile([P, SLOT_TILES], F32, name="ebf")
        fbf = keep.tile([P, SLOT_TILES], F32, name="fbf")
        cos_t = keep.tile([P, GROUPS, 32, 4], BF16, name="cos_t")
        sin_t = keep.tile([P, GROUPS, 32, 4], BF16, name="sin_t")

        x_codes = keep.tile([P, GROUPS, PASSES, 512], U32, name="x_codes", align_bytes=64)
        x_scales = keep.tile([P, GROUPS, PASSES, 512], U8, name="x_scales", align_bytes=64)
        e_codes = keep.tile([P, GROUPS, R], U32, name="e_codes", align_bytes=64)
        e_scales = keep.tile([P, GROUPS, R], U8, name="e_scales", align_bytes=64)
        f_codes = keep.tile([P, GROUPS, R], U32, name="f_codes", align_bytes=64)
        f_scales = keep.tile([P, GROUPS, R], U8, name="f_scales", align_bytes=64)
        kr_codes = keep.tile([P, GROUPS, D], U32, name="kr_codes", align_bytes=64)
        kr_scales = keep.tile([P, GROUPS, D], U8, name="kr_scales", align_bytes=64)
        vm_codes = keep.tile([P, GROUPS, D], U32, name="vm_codes", align_bytes=64)
        vm_scales = keep.tile([P, GROUPS, D], U8, name="vm_scales", align_bytes=64)
        w_codes = {}
        w_scales = {}
        for name in ("k", "v"):
            w_codes[name] = keep.tile([P, PASSES, D], U32, name="wc_" + name, align_bytes=64)
            w_scales[name] = keep.tile([P, PASSES, D], U8, name="ws_" + name, align_bytes=64)

        def new_tr():
            tr = psum.tile([P, 512], F32, name="tr", bufs=3)
            return tr

        def new_mm():
            mm = psum.tile([P, 512], F32, name="mm", bufs=3)
            return mm

        def new_acc():
            acc = psum.tile([P, 512], F32, name="acc", bufs=2)
            return acc

        def new_grp(kind):
            grp = work.tile([P, 512, 4], BF16, name="grp_" + kind, bufs=GRP_BUFS[kind], align_bytes=64)
            return grp

        def quantize(codes, scales, grp):
            nc.vector.quantize_mx(
                out=codes.bitcast(FP8X4), scales=scales, in_=grp[:].rearrange("p c t -> p (c t)")
            )

        def mx(out, lc, ls, rc, rs, start, stop):
            nc.tensor.matmul_mx(
                out=out, lhsT=lc.bitcast(FP8X4), lhsT_scale=ls, rhs=rc.bitcast(FP8X4), rhs_scale=rs,
                start=start, stop=stop,
            )

        f_wide = {}
        grps = {}
        mms = {}
        prods = {}
        c_t = {}
        vmts = {}
        accs = {}

        def grp_words(grp):
            return grp[:].rearrange("p c t -> p (c t)").bitcast(F32)

        def turn(words, bases, stride, bank=None):
            tr = new_tr() if bank is None else bank
            for n in range(4):
                nc.tensor.transpose(
                    tr[:, n * P : (n + 1) * P], words[:, bases[n] : bases[n] + stride * (P - 1) + 1 : stride], ident[:])
            return tr

        def interleave(dst, tr):
            nc.scalar.copy(dst.rearrange("p (c u) -> p c u", u=2), tr[:].rearrange("p (u c) -> p c u", u=2))

        def widen_f(g):
            fw = work.tile([P, SLOT_TILES, 512], BF16, name="fw", bufs=2, align_bytes=64)
            f_wide[g] = fw
            dst = fw[:].rearrange("p a k -> p (a k)")
            src = f_raw[g][:].rearrange("p a k -> p (a k)").bitcast(FP8)
            for cols in (slice(0, 1024), slice(1024, 2048)):
                nc.scalar.copy(dst[:, cols], src[:, cols])

        def f_turn(g, ap):
            words = f_wide[g][:].rearrange("p a k -> p (a k)").bitcast(F32)
            if F_ACT(g):
                prods["f", g, ap] = turn(words, [a * 256 + ap for a in range(4)], 2)
            else:
                bases = [(2 * ap + i) * 256 + u for u in range(2) for i in range(2)]
                prods["f", g, ap] = turn(words, bases, 2, new_mm())

        def f_planes(g, ap):
            if ap == 0:
                fpl = work.tile([P, 4, 512], BF16, name="fpl", bufs=2, align_bytes=64)
                prods["fpl", g] = fpl
            view = prods["f", g, ap][:].bitcast(BF16).rearrange("p (r i) -> p i r", i=2)
            for i in range(2):
                t = 2 * ap + i
                nc.scalar.activation(prods["fpl", g][:, t, :], view[:, i], ACTF.Copy, scale=fsc[:, g, t : t + 1])

        def f_mul(g, ap):
            if ap == 0:
                grps["f", g] = new_grp("f")
            if F_ACT(g):
                for part in range(2) if F_FINE else [0]:
                    cols = slice(ap * 256 + part * 128, ap * 256 + (part + 1) * 128) if F_FINE else slice(ap * 256, (ap + 1) * 256)
                    dst = grps["f", g][:, cols, :]
                    src = prods["fpl", g][:, :, cols].rearrange("p t r -> p r t")
                    if F_ENGINE(g, ap) == "gpsimd":
                        nc.gpsimd.tensor_scalar(dst, src, 1.0, 0.0, op0=ALU.mult, op1=ALU.add)
                    elif F_ENGINE(g, ap) == "vector":
                        nc.vector.tensor_copy(dst, src)
                    else:
                        nc.scalar.copy(dst, src)
                return
            nc.vector.tensor_tensor(
                grps["f", g][:, ap * 256 : (ap + 1) * 256, :].rearrange("p r (u i) -> p r u i", u=2),
                prods["f", g, ap][:].bitcast(BF16).rearrange("p (u r i) -> p r u i", u=2, i=2),
                fsc[:, g : g + 1, :].rearrange("p o (u i) -> p o u i", u=2).to_broadcast([P, 256, 2, 2]),
                op=ALU.mult,
            )

        def f_q(g):
            quantize(f_codes[:, g, :], f_scales[:, g, :], grps["f", g])

        def e_turn(g, ap):
            words = e_sb[g][:].rearrange("p a k -> p (a k)").bitcast(F32)
            prods["e", g, ap] = turn(words, [(2 * ap + i) * 256 + u for u in range(2) for i in range(2)], 2)

        def e_copy(g, ap):
            if ap == 0:
                grps["e", g] = new_grp("f")
            interleave(grp_words(grps["e", g])[:, ap * 512 : (ap + 1) * 512], prods["e", g, ap])

        def e_q(g):
            quantize(e_codes[:, g, :], e_scales[:, g, :], grps["e", g])

        def x_turn(g, kk, par):
            words = x_sb[g][:].rearrange("p t k -> p (t k)").bitcast(F32)
            bases = [(2 * s + par) * 512 + kk * 256 + u for u in range(2) for s in range(2)]
            prods["x", g, kk, par] = turn(words, bases, 2)

        def x_copy(g, kk, par):
            if par == 0:
                grps["x", g, kk] = new_grp("x")
            interleave(grp_words(grps["x", g, kk])[:, par * 512 : (par + 1) * 512], prods["x", g, kk, par])

        def x_q(g, kk):
            quantize(x_codes[:, g, kk, :], x_scales[:, g, kk, :], grps["x", g, kk])

        def w_pack(name, kk, part, engine):
            raw = w_raw[name]
            if part == 0:
                grps[name, kk] = new_grp("x")
            cols = slice(part * 256, (part + 1) * 256)
            if name == "k":
                dst = grps[name, kk][:, cols, :]
                src = raw[:, kk, :, cols].rearrange("p j c -> p c j")
            else:
                dst = grps[name, kk][:, cols, :].rearrange("p (i w) j -> p i w j", i=2)
                src = raw[:, kk, :, cols].rearrange("p j (w i) -> p i w j", i=2)
            if engine == "gpsimd":
                nc.gpsimd.tensor_scalar(dst, src, 1.0, 0.0, op0=ALU.mult, op1=ALU.add)
            elif engine == "vector":
                nc.vector.tensor_copy(dst, src)
            else:
                nc.scalar.copy(dst, src)

        def w_q(name, kk):
            quantize(w_codes[name][:, kk, :], w_scales[name][:, kk, :], grps[name, kk])

        def k_mm(g, hp):
            mm = new_mm()
            mms["k", g, hp] = mm
            for t in range(4):
                q = (t % 2) * 2 + t // 2
                for kk in range(PASSES):
                    mx(
                        mm[:, t * P : (t + 1) * P],
                        x_codes[:, g, kk, q * P : (q + 1) * P], x_scales[:, g, kk, q * P : (q + 1) * P],
                        w_codes["k"][:, kk, hp * P : (hp + 1) * P], w_scales["k"][:, kk, hp * P : (hp + 1) * P],
                        kk == 0, kk == PASSES - 1,
                    )

        def k_mul(g, hp):
            src = mms["k", g, hp][:].rearrange("p (t hh j) -> p hh j t", t=4, hh=4)
            if hp % 2 == 0:
                pc = work.tile([P, 2, 512], F32, name="pc", bufs=2)
                ps = work.tile([P, 2, 512], F32, name="ps", bufs=2)
                prods["k", g, hp // 2] = (pc, ps)
            pc, ps = prods["k", g, hp // 2]
            nc.vector.tensor_tensor(
                pc[:, hp % 2, :].rearrange("p (hh j t) -> p hh j t", hh=4, t=4), src,
                cos_t[:, g : g + 1].to_broadcast([P, 4, 32, 4]), op=ALU.mult)
            nc.vector.tensor_tensor(
                ps[:, hp % 2, :].rearrange("p (hh j t) -> p hh j t", hh=4, t=4), src,
                sin_t[:, g : g + 1].to_broadcast([P, 4, 32, 4]), op=ALU.mult)

        def k_add(g, hp):
            if hp == 0:
                grps["kr", g] = new_grp("kr")
            pc, ps = prods["k", g, hp]
            flat = grps["kr", g][:].rearrange("p c t -> p (c t)")
            eng = nc.gpsimd if ADD_ENGINE(g, hp) else nc.vector
            dst = flat[:, hp * 1024 : (hp + 1) * 1024].rearrange("p (h b n) -> p h b n", h=4, b=2)
            pcv = pc[:].rearrange("p q (h b n) -> p (q h) b n", h=2, b=2)
            psv = ps[:].rearrange("p q (h b n) -> p (q h) b n", h=2, b=2)
            eng.tensor_tensor(dst[:, :, 0, :], pcv[:, :, 0, :], psv[:, :, 1, :], op=ALU.subtract)
            eng.tensor_tensor(dst[:, :, 1, :], pcv[:, :, 1, :], psv[:, :, 0, :], op=ALU.add)

        def kr_q(g):
            quantize(kr_codes[:, g, :], kr_scales[:, g, :], grps["kr", g])

        def v0_turn(g, dd):
            words = v0_sb[g][:].rearrange("p t d -> p (t d)").bitcast(F32)
            prods["v0", g, dd] = turn(words, [t * 256 + dd * P for t in (0, 2, 1, 3)], 1)

        def v0_scale(g, dd):
            ct = work.tile([P, 2, 512], F32, name="ct", bufs=3)
            c_t[g, dd] = ct
            view = prods["v0", g, dd][:].bitcast(BF16).rearrange("p (par c i) -> p i c par", par=2, i=2)
            for i in range(2):
                ft = 2 * dd + i
                nc.scalar.activation(
                    ct[:, i, :].rearrange("p (c par) -> p c par", par=2), view[:, i],
                    ACTF.Copy, scale=oml[:, ft : ft + 1])

        def v_mm(g, ft):
            mm = new_mm()
            mms["v", g, ft] = mm
            for kk in range(PASSES):
                mx(
                    mm[:],
                    w_codes["v"][:, kk, ft * P : (ft + 1) * P], w_scales["v"][:, kk, ft * P : (ft + 1) * P],
                    x_codes[:, g, kk, :], x_scales[:, g, kk, :],
                    kk == 0, kk == PASSES - 1,
                )

        def v_mix(g, ft):
            if ft == 0:
                vmt = work.tile([P, 4, 512], BF16, name="vmt", bufs=2, align_bytes=64)
                vmts[g] = vmt
            nc.vector.scalar_tensor_tensor(
                vmts[g][:, ft, :].rearrange("p (c par) -> p c par", par=2),
                mms["v", g, ft][:].rearrange("p (par c) -> p c par", par=2),
                lamf[:, ft : ft + 1],
                c_t[g, ft // 2][:, ft % 2, :].rearrange("p (c par) -> p c par", par=2),
                op0=ALU.mult, op1=ALU.add,
            )

        def vm_turn(g, dd):
            words = vmts[g][:].rearrange("p f c -> p (f c)").bitcast(F32)
            prods["vm", g, dd] = turn(words, [(2 * dd + i) * 256 + u * P for u in range(2) for i in range(2)], 1)

        def vm_copy(g, dd):
            if dd == 0:
                grps["vm", g] = new_grp("vm")
            interleave(grp_words(grps["vm", g])[:, dd * 512 : (dd + 1) * 512], prods["vm", g, dd])

        def vm_q(g):
            quantize(vm_codes[:, g, :], vm_scales[:, g, :], grps["vm", g])

        out_k = out_0.rearrange("(p a) d -> a p d", a=SLOT_TILES)
        out_v = out_1.rearrange("(p a) d -> a p d", a=SLOT_TILES)

        def ks_mm(a):
            accs["k", a] = new_acc()
            cols = slice(a * P, (a + 1) * P)
            for g in range(GROUPS):
                mx(accs["k", a][:], e_codes[:, g, cols], e_scales[:, g, cols], kr_codes[:, g, :], kr_scales[:, g, :],
                   g == 0, g == GROUPS - 1)

        def ks_sq(a):
            ss = work.tile([P, H], F32, name="ss", bufs=2)
            for h in range(H):
                sq = work.tile([P, C], F32, name="sq", bufs=2)
                nc.scalar.activation(
                    sq[:], accs["k", a][:, h * C : (h + 1) * C], ACTF.Square, bias=ebf[:, a : a + 1],
                    accum_out=ss[:, h : h + 1])
            prods["ss", a] = ss

        def ks_read(a):
            yg = work.tile([P, H, C], F32, name="res", bufs=6)
            nc.vector.scalar_tensor_tensor(
                yg[:].rearrange("p h c -> p (h c)"), accs["k", a][:], ebf[:, a : a + 1], gain_sb[:],
                op0=ALU.add, op1=ALU.mult)
            prods["yg", a] = yg

        def ks_norm(a):
            rt = work.tile([P, H], F32, name="rt", bufs=2)
            nc.scalar.activation(rt[:], prods["ss", a][:], ACTF.Sqrt, bias=eps_col[:], scale=1.0 / C)
            prods["rt", a] = rt

        def ks_rec(a):
            ri = work.tile([P, H], F32, name="ri", bufs=2)
            nc.vector.reciprocal(ri[:], prods["rt", a][:])
            prods["ri", a] = ri

        def ks_out(a):
            yg = prods["yg", a]
            ri = prods["ri", a]
            if KO == "act":
                for h in range(H):
                    nc.scalar.activation(yg[:, h, :], yg[:, h, :], ACTF.Copy, scale=ri[:, h : h + 1])
            else:
                nc.vector.tensor_tensor(
                    yg[:], yg[:], ri[:].rearrange("p (h o) -> p h o", o=1).to_broadcast([P, H, C]), op=ALU.mult)
            nc.sync.dma_start(out=out_k[a], in_=yg[:].rearrange("p h c -> p (h c)"))

        def vs_mm(a, g):
            if g == 0:
                accs["v", a] = new_acc() if a < 2 else new_mm()
            cols = slice(a * P, (a + 1) * P)
            mx(accs["v", a][:], f_codes[:, g, cols], f_scales[:, g, cols], vm_codes[:, g, :], vm_scales[:, g, :],
               g == 0, g == GROUPS - 1)

        def vs_out(a):
            vo = work.tile([P, D], F32, name="res", bufs=6)
            dst = vo[:].rearrange("p (dd w i) -> p dd w i", dd=2, i=2)
            src = accs["v", a][:].rearrange("p (dd i w) -> p dd w i", dd=2, i=2)
            if VS_ACT(a):
                nc.scalar.activation(dst, src, ACTF.Identity, bias=fbf[:, a : a + 1])
            else:
                nc.vector.tensor_scalar(dst, src, fbf[:, a : a + 1], None, op0=ALU.add)
            nc.sync.dma_start(out=out_v[a], in_=vo[:])

        def tables():
            nc.scalar.copy(cos_t[:], cos_raw[:].rearrange("p g t j -> p g j t"))
            nc.scalar.copy(sin_t[:], sin_raw[:].rearrange("p g t j -> p g j t"))

        def columns():
            nc.gpsimd.tensor_copy(lamf[:], lam_raw[:].rearrange("p a i -> p (a i)"))
            nc.gpsimd.tensor_scalar(oml[:], lamf[:], -1.0, 1.0, op0=ALU.mult, op1=ALU.add)
            nc.gpsimd.tensor_copy(ebf[:], eb_raw[:])
            nc.gpsimd.tensor_copy(fbf[:], fb_raw[:])

        ALL = []
        for kind, count in (("f", 4), ("x0", 2), ("wk", 2), ("wv", 2), ("v0", 4), ("e", 4), ("small", 7)):
            for i in range(count):
                ALL.append(("ld_" + kind, (i,), loaders[kind]))
        for i in range(1, 4):
            ALL.append(("ld_x", (i,), load_x))
        ALL.append(("tables", (), tables))
        ALL.append(("columns", (), columns))
        for g in range(GROUPS):
            ALL.append(("f_wid", (g,), widen_f))
        for g in range(GROUPS):
            for ap in range(2):
                ALL.append(("f_turn", (g, ap), f_turn))
                ALL.append(("f_mul", (g, ap), f_mul))
                ALL.append(("e_turn", (g, ap), e_turn))
                ALL.append(("v0_turn", (g, ap), v0_turn))
                ALL.append(("vm_turn", (g, ap), vm_turn))
                ALL.append(("e_copy", (g, ap), e_copy))
                ALL.append(("v0_scale", (g, ap), v0_scale))
                ALL.append(("vm_copy", (g, ap), vm_copy))
                if F_ACT(g):
                    ALL.append(("f_scale", (g, ap), f_planes))
                for kk in range(2):
                    ALL.append(("x_turn", (g, kk, ap), x_turn))
                    ALL.append(("x_copy", (g, kk, ap), x_copy))
            ALL.append(("f_q", (g,), f_q))
            ALL.append(("e_q", (g,), e_q))
            ALL.append(("kr_q", (g,), kr_q))
            ALL.append(("vm_q", (g,), vm_q))
            for kk in range(2):
                ALL.append(("x_q", (g, kk), x_q))
            for hp in range(4):
                ALL.append(("k_mm", (g, hp), k_mm))
                ALL.append(("k_mul", (g, hp), k_mul))
                if hp < 2:
                    ALL.append(("k_add", (g, hp), k_add))
                ALL.append(("v_mm", (g, hp), v_mm))
                ALL.append(("v_mix", (g, hp), v_mix))
                ALL.append(("vs_mm", (hp, g), vs_mm))
        for a in range(4):
            ALL.append(("ks_mm", (a,), ks_mm))
            ALL.append(("ks_sq", (a,), ks_sq))
            ALL.append(("ks_read", (a,), ks_read))
            ALL.append(("ks_norm", (a,), ks_norm))
            ALL.append(("ks_rec", (a,), ks_rec))
            ALL.append(("ks_out", (a,), ks_out))
            ALL.append(("vs_out", (a,), vs_out))
        for name in ("k", "v"):
            for kk in range(2):
                for part in range(2):
                    ALL.append(("w_pack_" + name, (kk, part), lambda kk, part, name=name: w_pack(name, kk, part, W_ENGINE[name, kk, part])))
                ALL.append(("w_q_" + name, (kk,), lambda kk, name=name: w_q(name, kk)))
        table = {}
        for kind, idx, fn in ALL:
            table[":".join([kind] + [str(i) for i in idx])] = (fn, idx)
        words_of_order = ORDER.split()
        assert len(words_of_order) == len(ALL)
        for word in words_of_order:
            fn, idx = table[word]
            fn(*idx)
